import numpy as np
import ml_dtypes


def mxq(x, axis, fmt="e4m3"):
    dtype, down = {"e4m3": (ml_dtypes.float8_e4m3fn, 7), "e5m2": (ml_dtypes.float8_e5m2, 14)}[fmt]
    v = np.moveaxis(np.asarray(x, np.float32).astype(ml_dtypes.bfloat16).astype(np.float64), axis, -1)
    blocks = v.reshape(v.shape[:-1] + (-1, 32))
    amax = np.abs(blocks).max(-1, keepdims=True)
    byte = np.maximum(np.where(amax > 0, np.frexp(amax)[1] - 1 + 127, 0) - down, 1)
    scale = np.exp2(byte - 127.0)
    codes = (blocks / scale).astype(np.float32).astype(dtype).astype(np.float64)
    return np.moveaxis((codes * scale).reshape(v.shape), -1, axis)


WIDE = False


def mx_kscale(k):
    if not WIDE:
        return np.ones(k)
    levels = np.array([10, -10, 5, -5, 0])
    if k % 512:
        return np.exp2(np.random.permutation(np.resize(levels, k // 32))).repeat(32)
    a = np.empty((k // 512, 16))
    for p in range(k // 512):
        a[p, :8] = np.random.permutation(np.resize(levels, 8))
        for g in range(8):
            far = levels[np.abs(levels - a[p, g]) >= 10]
            a[p, g + 8] = far[np.random.randint(len(far))]
    return np.exp2(a.ravel()).repeat(32)


def f64(x):
    return np.asarray(x).astype(np.float64)


def striped(idx):
    return np.tile(idx.reshape(-1, 16).T, (8, 1)).astype(np.uint16)


def unstriped(offs):
    return offs[:16].T.reshape(-1).astype(np.int64)


def striped8(idx):
    return np.concatenate([x.reshape(-1, 16).T for x in idx]).astype(np.uint16)


def runs(offs, k):
    lists = np.stack([offs[16 * r : 16 * r + 16].T.reshape(-1) for r in range(8)]).astype(np.int64)
    return lists[np.arange(k) % 512 // 64]


def pack_weight(w):
    k, n = w.shape
    w = f64(np.asarray(w, np.float32).astype(ml_dtypes.bfloat16)).reshape(k // 32, 32, n)
    amax = np.abs(w).max(1)
    byte = np.clip(np.where(amax > 0, np.frexp(amax)[1] - 1 + 127 - 7, 1), 1, 254)
    scaled = (w * np.exp2(127.0 - byte)[:, None, :]).reshape(k, n).astype(np.float32)
    words = np.ascontiguousarray(scaled.reshape(k // 512, 128, 4, n).transpose(0, 1, 3, 2)).astype(ml_dtypes.float8_e4m3fn).view(np.uint8)
    return words, np.ascontiguousarray(byte.astype(np.uint8).reshape(k // 512, 16, n))


def unpack_weight(words, scales):
    g, p, n, _ = words.shape
    vals = np.ascontiguousarray(words).view(ml_dtypes.float8_e4m3fn).astype(np.float64) * np.repeat(np.exp2(scales.astype(np.float64) - 127.0), 8, axis=1)[..., None]
    return vals.transpose(0, 1, 3, 2).reshape(g * 512, n)


K, T, S, G, H, C, U = 512, 1024, 512, 2048, 512, 512, 1024


def setup_inputs():
    n = np.random.standard_normal
    s = mx_kscale(K)[:, None]
    packed_xT = pack_weight(n((K, T)) * s)
    packed_dT = pack_weight(n((K, G)) / s)
    return {
        "x_words": packed_xT[0],
        "x_scales": packed_xT[1],
        "d_words": packed_dT[0],
        "d_scales": packed_dT[1],
        "gs": (np.random.uniform(0.5, 1.5, (K, 1)) / s).astype(np.float32),
        "mem": n((C, U)).astype(np.float32),
        "offs": striped(np.random.permutation(T)[:S]),
        "k1": striped8(np.random.randint(0, G, (8, H))),
        "n1": striped8(np.stack([np.random.permutation(S) for _ in range(8)])),
        "cand": striped(np.random.permutation(T)[:C]),
        "n2": striped8(np.stack([np.random.permutation(U)[:S] for _ in range(8)])),
    }


def reference(x_words, x_scales, d_words, d_scales, gs, mem, offs, k1, n1, cand, n2):
    x_cand = unpack_weight(x_words, x_scales)[:, unstriped(cand)]
    d_k1 = unpack_weight(d_words, d_scales)[np.arange(K)[:, None], runs(k1, K)]
    xq = unpack_weight(x_words, x_scales)[:, unstriped(offs)]
    h = 0.0625 * (d_k1.T @ xq)
    pa = h[np.arange(H)[:, None], runs(n1, H)]
    z = f64(gs) * ((2.0 * (h * pa)) / ((h) ** 2 + (pa) ** 2 + 0.5))
    s = 0.0625 * ((x_cand.T @ mxq(z, 0, "e4m3")))
    nw = np.maximum(s, 0.5 * (f64(mem)[np.arange(C)[:, None], runs(n2, C)]))
    out = f64(mem).copy()
    out[np.arange(C)[:, None], runs(n2, C)] = nw
    return out

@@ -1,0 +1,216 @@
+from contextlib import ExitStack
+
+import concourse.mybir as mybir
+from concourse.masks import make_identity
+
+F32 = mybir.dt.float32
+BF16 = mybir.dt.bfloat16
+I32 = mybir.dt.int32
+U32 = mybir.dt.uint32
+U16 = mybir.dt.uint16
+U8 = mybir.dt.uint8
+FP8X4 = mybir.dt.float8_e4m3fn_x4
+ACT = mybir.ActivationFunctionType
+ALU = mybir.AluOpType
+
+P = 128
+PACK = 4
+T, G, U = 1024, 2048, 1024
+S = 512
+FLOPS = 2 * 2 * 512 * 512 * 512
+
+
+def tile_picked_pqcharmpagex_none_p_kernel(
+    tc, x_words, x_scales, d_words, d_scales, gs, mem, offs, k1, n1, cand, n2, out
+):
+    nc = tc.nc
+    with ExitStack() as ctx:
+        keep = ctx.enter_context(tc.tile_pool(name="keep", bufs=1))
+        psum = ctx.enter_context(tc.psum_pool(name="psum", bufs=1))
+
+        def load_list(src, name):
+            tile = keep.tile([P, S // 16], U16, name=name)
+            nc.sync.dma_start(tile[:], src)
+            return tile
+
+        def dealt(ap):
+            return ap.rearrange("p (t m) -> p m t", t=PACK)
+
+        def in_order(ap):
+            return ap.rearrange("p (m t) -> p m t", t=PACK)
+
+        d_byte_table = keep.tile([P, G], U8, align_bytes=64)
+        x_byte_table = keep.tile([P, T], U8, align_bytes=64)
+        planes = keep.tile([P, 3 * S], U8, align_bytes=64)
+        nc.vector.memset(planes[:].bitcast(I32), 0)
+
+        k1_list = load_list(k1, "k1_list")
+        nc.sync.dma_start(d_byte_table[:].bitcast(I32), d_scales[0].bitcast(I32).unsqueeze(1).broadcast_to([16, 8, G // 4]))
+        cand_list = load_list(cand, "cand_list")
+        nc.sync.dma_start(x_byte_table[:].bitcast(I32), x_scales[0].bitcast(I32).unsqueeze(1).broadcast_to([16, 8, T // 4]))
+        offs_list = load_list(offs, "offs_list")
+        d_word_table = keep.tile([P, G], U32, align_bytes=64)
+        nc.sync.dma_start(d_word_table[:].bitcast(I32), d_words[0].rearrange("p n t -> p (n t)").bitcast(I32))
+        x_word_table = keep.tile([P, T], U32, align_bytes=64)
+        nc.sync.dma_start(x_word_table[:].bitcast(I32), x_words[0].rearrange("p n t -> p (n t)").bitcast(I32))
+        n1_list = load_list(n1, "n1_list")
+        n2_list = load_list(n2, "n2_list")
+        gain = keep.tile([P, PACK], F32)
+        nc.sync.dma_start(gain[:], gs.rearrange("(p t) o -> p (t o)", t=PACK))
+        mem_rows = mem.rearrange("(p t) w -> t p w", t=PACK)
+        out_rows = out.rearrange("(p t) w -> t p w", t=PACK)
+        pages = []
+
+        def load_page(slot):
+            t = len(pages)
+            pages.append(keep.tile([P, U], F32, name=f"page{t}", tag=slot, align_bytes=64))
+            nc.sync.dma_start(pages[t][:], mem_rows[t])
+
+        identity = keep.tile([P, P], F32)
+        make_identity(nc, identity[:])
+
+        picked_bytes = keep.tile([P, 3 * S], U8, tag="picked", align_bytes=64)
+        nc.vector.tensor_copy(picked_bytes[:, 0:S], d_byte_table[:].indirect(k1_list[:]))
+        nc.vector.tensor_copy(picked_bytes[:, S : 2 * S], x_byte_table[:].indirect(cand_list[:]))
+        nc.vector.tensor_copy(picked_bytes[:, 2 * S : 3 * S], x_byte_table[:].indirect(offs_list[:]))
+        load_page("d_byte_table")
+        for r in range(4):
+            nc.scalar.dma_start(planes[r:P:32, :].bitcast(I32), picked_bytes[8 * r : P : 32, :].bitcast(I32))
+
+        d_picked = keep.tile([P, S], U32, align_bytes=64)
+        nc.vector.tensor_copy(d_picked[:], d_word_table[:].indirect(k1_list[:]))
+        xq_words = keep.tile([P, S], U32, align_bytes=64)
+        nc.vector.tensor_copy(xq_words[:], x_word_table[:].indirect(offs_list[:]))
+        d_dealt = keep.tile([P, S], U32, align_bytes=64)
+        nc.vector.tensor_copy(dealt(d_dealt[:]), in_order(d_picked[:]))
+        load_page("d_word_table")
+        load_page("d_picked")
+        d_plane = keep.tile([P, S], U8, align_bytes=64)
+        nc.vector.tensor_copy(dealt(d_plane[:]), in_order(planes[:, 0:S]))
+
+        h_banks = []
+        for t in range(PACK):
+            cols = slice(t * P, (t + 1) * P)
+            bank = psum.tile([P, S], F32, name=f"h_bank{t}", tag=f"first{t}")
+            nc.tensor.matmul_mx(
+                out=bank[:],
+                lhsT=d_dealt[:, cols].bitcast(FP8X4),
+                lhsT_scale=d_plane[:, cols],
+                rhs=xq_words[:].bitcast(FP8X4),
+                rhs_scale=planes[:, 2 * S : 3 * S],
+                start=True,
+                stop=True,
+            )
+            h_banks.append(bank)
+
+        c_picked = keep.tile([P, S], U32, tag="picked", align_bytes=64)
+        nc.vector.tensor_copy(c_picked[:], x_word_table[:].indirect(cand_list[:]))
+        load_page("x_word_table")
+        c_plane = keep.tile([P, S], U8, align_bytes=64)
+        nc.vector.tensor_copy(dealt(c_plane[:]), in_order(planes[:, S : 2 * S]))
+        c_dealt = keep.tile([P, S], U32, align_bytes=64)
+        nc.vector.tensor_copy(dealt(c_dealt[:]), in_order(c_picked[:]))
+
+        h_tiles = [keep.tile([P, 2 * S], F32, name=f"h{t}", align_bytes=64) for t in range(PACK)]
+        pa = [keep.tile([P, S], F32, name=f"pa{t}", align_bytes=64) for t in range(PACK)]
+        pa_sq = [keep.tile([P, S], F32, name=f"pa_sq{t}", align_bytes=64) for t in range(PACK)]
+        root = [keep.tile([P, S], F32, name=f"root{t}") for t in range(PACK)]
+        recip = [keep.tile([P, S], F32, name=f"recip{t}") for t in range(PACK)]
+        halves = []
+        numer = keep.tile([P, PACK, S], F32)
+        sum_banks = [psum.tile([P, PACK, P], F32, name=f"sum_bank{c}", tag=f"second{c}") for c in range(PACK)]
+
+        def evacuate(t):
+            nc.scalar.activation(h_tiles[t][:, 0:S], h_banks[t][:], ACT.Copy, scale=0.0625)
+            nc.scalar.activation(h_tiles[t][:, S : 2 * S], h_banks[t][:], ACT.Square, scale=0.0625)
+
+        def look_up(t):
+            nc.vector.tensor_copy(pa[t][:], h_tiles[t][:].indirect(n1_list[:]))
+            nc.scalar.activation(pa_sq[t][:], pa[t][:], ACT.Square)
+
+        def add_squares(t):
+            for c in range(PACK):
+                cols = slice(c * P, (c + 1) * P)
+                nc.tensor.matmul(sum_banks[c][:, t, :], h_tiles[t][:, S + c * P : S + (c + 1) * P], identity[:],
+                                 start=True, stop=False, is_transpose=True)
+                nc.tensor.matmul(sum_banks[c][:, t, :], pa_sq[t][:, cols], identity[:],
+                                 start=False, stop=True, is_transpose=True)
+
+        def invert(t):
+            nc.scalar.activation(root[t][:], sum_banks[t][:].rearrange("j t p -> j (t p)"), ACT.Abs_reciprocal_sqrt, scale=0.5, bias=0.25)
+            nc.scalar.activation(recip[t][:], root[t][:], ACT.Square)
+
+        def numerator(t):
+            nc.vector.scalar_tensor_tensor(numer[:, t, :], pa[t][:], gain[:, t : t + 1], h_tiles[t][:, 0:S], ALU.mult, ALU.mult)
+
+        def fetch_half(t, slot):
+            halves.append(keep.tile([P, S], F32, name=f"half{t}", tag=slot, align_bytes=64))
+            nc.vector.tensor_scalar(halves[t][:], pages[t][:].indirect(n2_list[:]), 0.5, 0.0, ALU.mult, ALU.add)
+
+        evacuate(0)
+        evacuate(1)
+        for t in range(PACK):
+            look_up(t)
+            add_squares(t)
+            if t + 2 < PACK:
+                evacuate(t + 2)
+            if t >= 1:
+                numerator(t - 1)
+        numerator(PACK - 1)
+        for t, slot in enumerate(("pa3", "pa_sq3", "h3")):
+            fetch_half(t, slot)
+
+        recip_banks = [psum.tile([P, PACK, P], F32, name=f"recip_bank{c}", tag=f"first{c}") for c in range(PACK)]
+        for c in range(PACK):
+            invert(c)
+            for t in range(PACK):
+                nc.tensor.transpose(recip_banks[c][:, t, :], recip[c][:, t * P : (t + 1) * P], identity[:])
+
+        z = [keep.tile([P, S // 2, PACK], BF16, name=f"z{i}", align_bytes=64) for i in range(2)]
+        z_words = [keep.tile([P, S // 2], U32, name=f"z_words{i}", align_bytes=64) for i in range(2)]
+        z_plane = [keep.tile([P, S // 2], U8, name=f"z_plane{i}", align_bytes=64) for i in range(2)]
+
+        def finish_z(c):
+            nc.vector.tensor_tensor(
+                z[c // 2][:, (c % 2) * P : (c % 2 + 1) * P, :],
+                numer[:, :, c * P : (c + 1) * P].rearrange("p t j -> p j t"),
+                recip_banks[c][:].rearrange("p t j -> p j t"),
+                ALU.mult,
+            )
+
+        def quantise(i):
+            nc.vector.quantize_mx(out=z_words[i][:].bitcast(FP8X4), scales=z_plane[i][:], in_=z[i][:].rearrange("p j t -> p (j t)"))
+
+        finish_z(0)
+        finish_z(1)
+        finish_z(2)
+        quantise(0)
+        finish_z(3)
+        quantise(1)
+        fetch_half(PACK - 1, "z1")
+
+        s_banks = [psum.tile([P, S], F32, name=f"s_bank{t}", tag=f"second{t}") for t in range(PACK)]
+        for i in range(2):
+            for t in range(PACK):
+                cols = slice(t * P, (t + 1) * P)
+                nc.tensor.matmul_mx(
+                    out=s_banks[t][:, i * (S // 2) : (i + 1) * (S // 2)],
+                    lhsT=c_dealt[:, cols].bitcast(FP8X4),
+                    lhsT_scale=c_plane[:, cols],
+                    rhs=z_words[i][:].bitcast(FP8X4),
+                    rhs_scale=z_plane[i][:],
+                    start=True,
+                    stop=True,
+                )
+
+        larger = [keep.tile([P, S], F32, name=f"larger{t}") for t in range(PACK)]
+
+        def take_larger(t):
+            nc.vector.scalar_tensor_tensor(larger[t][:], s_banks[t][:], 0.0625, halves[t][:], ALU.mult, ALU.max)
+
+        take_larger(0)
+        for t in range(PACK):
+            if t + 1 < PACK:
+                take_larger(t + 1)
+            nc.vector.tensor_copy(pages[t][:].indirect(n2_list[:]), larger[t][:])
+            nc.sync.dma_start(out_rows[t], pages[t][:])

@@ -41,22 +41,25 @@ def tile_picked_pqcharmpagex_none_p_kernel(
 
         d_byte_table = keep.tile([P, G], U8, align_bytes=64)
         x_byte_table = keep.tile([P, T], U8, align_bytes=64)
-        planes = keep.tile([P, 3 * S], U8, align_bytes=64)
+        planes = keep.tile([P, 2 * S], U8, align_bytes=64)
+        c_rows = keep.tile([P, S], U8, align_bytes=64)
+        warm = keep.tile([P, 2], F32)
+        nc.vector.memset(warm[:, 0:1], 1.0)
+        nc.scalar.activation(warm[:, 1:2], warm[:, 0:1], ACT.Abs_reciprocal_sqrt)
         nc.vector.memset(planes[:].bitcast(I32), 0)
+        nc.vector.memset(c_rows[:].bitcast(I32), 0)
 
         k1_list = load_list(k1, "k1_list")
         nc.sync.dma_start(d_byte_table[:].bitcast(I32), d_scales[0].bitcast(I32).unsqueeze(1).broadcast_to([16, 8, G // 4]))
-        cand_list = load_list(cand, "cand_list")
-        nc.sync.dma_start(x_byte_table[:].bitcast(I32), x_scales[0].bitcast(I32).unsqueeze(1).broadcast_to([16, 8, T // 4]))
         offs_list = load_list(offs, "offs_list")
-        d_word_table = keep.tile([P, G], U32, align_bytes=64)
-        nc.sync.dma_start(d_word_table[:].bitcast(I32), d_words[0].rearrange("p n t -> p (n t)").bitcast(I32))
-        x_word_table = keep.tile([P, T], U32, align_bytes=64)
-        nc.sync.dma_start(x_word_table[:].bitcast(I32), x_words[0].rearrange("p n t -> p (n t)").bitcast(I32))
+        nc.sync.dma_start(x_byte_table[:].bitcast(I32), x_scales[0].bitcast(I32).unsqueeze(1).broadcast_to([16, 8, T // 4]))
+        cand_list = load_list(cand, "cand_list")
         n1_list = load_list(n1, "n1_list")
         n2_list = load_list(n2, "n2_list")
-        gain = keep.tile([P, PACK], F32)
-        nc.sync.dma_start(gain[:], gs.rearrange("(p t) o -> p (t o)", t=PACK))
+        x_word_table = keep.tile([P, T], U32, align_bytes=64)
+        nc.sync.dma_start(x_word_table[:].bitcast(I32), x_words[0].rearrange("p n t -> p (n t)").bitcast(I32))
+        d_word_table = keep.tile([P, G], U32, align_bytes=64)
+        nc.sync.dma_start(d_word_table[:].bitcast(I32), d_words[0].rearrange("p n t -> p (n t)").bitcast(I32))
         mem_rows = mem.rearrange("(p t) w -> t p w", t=PACK)
         out_rows = out.rearrange("(p t) w -> t p w", t=PACK)
         pages = []
@@ -69,23 +72,22 @@ def tile_picked_pqcharmpagex_none_p_kernel(
         identity = keep.tile([P, P], F32)
         make_identity(nc, identity[:])
 
-        picked_bytes = keep.tile([P, 3 * S], U8, tag="picked", align_bytes=64)
+        picked_bytes = keep.tile([P, 2 * S], U8, align_bytes=64)
         nc.vector.tensor_copy(picked_bytes[:, 0:S], d_byte_table[:].indirect(k1_list[:]))
-        nc.vector.tensor_copy(picked_bytes[:, S : 2 * S], x_byte_table[:].indirect(cand_list[:]))
-        nc.vector.tensor_copy(picked_bytes[:, 2 * S : 3 * S], x_byte_table[:].indirect(offs_list[:]))
-        load_page("d_byte_table")
+        nc.vector.tensor_copy(picked_bytes[:, S : 2 * S], x_byte_table[:].indirect(offs_list[:]))
+        gain = keep.tile([P, PACK], F32, tag="d_byte_table", align_bytes=64)
+        nc.sync.dma_start(gain[:], gs.rearrange("(p t) o -> p (t o)", t=PACK))
         for r in range(4):
             nc.scalar.dma_start(planes[r:P:32, :].bitcast(I32), picked_bytes[8 * r : P : 32, :].bitcast(I32))
+        load_page("picked_bytes")
 
-        d_picked = keep.tile([P, S], U32, align_bytes=64)
-        nc.vector.tensor_copy(d_picked[:], d_word_table[:].indirect(k1_list[:]))
         xq_words = keep.tile([P, S], U32, align_bytes=64)
         nc.vector.tensor_copy(xq_words[:], x_word_table[:].indirect(offs_list[:]))
+        d_picked = keep.tile([P, S], U32, align_bytes=64)
+        nc.vector.tensor_copy(d_picked[:], d_word_table[:].indirect(k1_list[:]))
         d_dealt = keep.tile([P, S], U32, align_bytes=64)
         nc.vector.tensor_copy(dealt(d_dealt[:]), in_order(d_picked[:]))
-        load_page("d_word_table")
-        load_page("d_picked")
-        d_plane = keep.tile([P, S], U8, align_bytes=64)
+        d_plane = keep.tile([P, S], U8, tag="d_word_table", align_bytes=64)
         nc.vector.tensor_copy(dealt(d_plane[:]), in_order(planes[:, 0:S]))
 
         h_banks = []
@@ -97,27 +99,28 @@ def tile_picked_pqcharmpagex_none_p_kernel(
                 lhsT=d_dealt[:, cols].bitcast(FP8X4),
                 lhsT_scale=d_plane[:, cols],
                 rhs=xq_words[:].bitcast(FP8X4),
-                rhs_scale=planes[:, 2 * S : 3 * S],
+                rhs_scale=planes[:, S : 2 * S],
                 start=True,
                 stop=True,
             )
             h_banks.append(bank)
 
-        c_picked = keep.tile([P, S], U32, tag="picked", align_bytes=64)
+        c_bytes = keep.tile([P, S], U8, tag="d_picked", align_bytes=64)
+        nc.vector.tensor_copy(c_bytes[:], x_byte_table[:].indirect(cand_list[:]))
+        for r in range(4):
+            nc.sync.dma_start(c_rows[r:P:32, :].bitcast(I32), c_bytes[8 * r : P : 32, :].bitcast(I32))
+        c_picked = keep.tile([P, S], U32, tag="x_byte_table", align_bytes=64)
         nc.vector.tensor_copy(c_picked[:], x_word_table[:].indirect(cand_list[:]))
+        load_page("d_dealt")
+        load_page("xq_words")
         load_page("x_word_table")
-        c_plane = keep.tile([P, S], U8, align_bytes=64)
-        nc.vector.tensor_copy(dealt(c_plane[:]), in_order(planes[:, S : 2 * S]))
-        c_dealt = keep.tile([P, S], U32, align_bytes=64)
-        nc.vector.tensor_copy(dealt(c_dealt[:]), in_order(c_picked[:]))
 
         h_tiles = [keep.tile([P, 2 * S], F32, name=f"h{t}", align_bytes=64) for t in range(PACK)]
         pa = [keep.tile([P, S], F32, name=f"pa{t}", align_bytes=64) for t in range(PACK)]
         pa_sq = [keep.tile([P, S], F32, name=f"pa_sq{t}", align_bytes=64) for t in range(PACK)]
-        root = [keep.tile([P, S], F32, name=f"root{t}") for t in range(PACK)]
+        root = [keep.tile([P, S], F32, name=f"root{t}", align_bytes=64) for t in range(PACK)]
         recip = [keep.tile([P, S], F32, name=f"recip{t}") for t in range(PACK)]
         halves = []
-        numer = keep.tile([P, PACK, S], F32)
         sum_banks = [psum.tile([P, PACK, P], F32, name=f"sum_bank{c}", tag=f"second{c}") for c in range(PACK)]
 
         def evacuate(t):
@@ -150,15 +153,19 @@ def tile_picked_pqcharmpagex_none_p_kernel(
         evacuate(0)
         evacuate(1)
         for t in range(PACK):
-            look_up(t)
-            add_squares(t)
             if t + 2 < PACK:
                 evacuate(t + 2)
-            if t >= 1:
-                numerator(t - 1)
-        numerator(PACK - 1)
-        for t, slot in enumerate(("pa3", "pa_sq3", "h3")):
-            fetch_half(t, slot)
+            look_up(t)
+            add_squares(t)
+        numer = keep.tile([P, PACK, S], F32, tag="pa_sq1", align_bytes=64)
+        for t in range(PACK):
+            numerator(t)
+        fetch_half(0, "pa_sq2")
+        c_dealt = keep.tile([P, S], U32, tag="pa_sq3", align_bytes=64)
+        nc.vector.tensor_copy(dealt(c_dealt[:]), in_order(c_picked[:]))
+        c_plane = keep.tile([P, S], U8, tag="pa0", align_bytes=64)
+        nc.vector.tensor_copy(dealt(c_plane[:]), in_order(c_rows[:]))
+        fetch_half(1, "pa1")
 
         recip_banks = [psum.tile([P, PACK, P], F32, name=f"recip_bank{c}", tag=f"first{c}") for c in range(PACK)]
         for c in range(PACK):
@@ -183,6 +190,7 @@ def tile_picked_pqcharmpagex_none_p_kernel(
 
         finish_z(0)
         finish_z(1)
+        fetch_half(2, "root0")
         finish_z(2)
         quantise(0)
         finish_z(3)

from contextlib import ExitStack

import concourse.mybir as mybir
from concourse.masks import make_identity

F32 = mybir.dt.float32
BF16 = mybir.dt.bfloat16
I32 = mybir.dt.int32
U32 = mybir.dt.uint32
U16 = mybir.dt.uint16
U8 = mybir.dt.uint8
FP8X4 = mybir.dt.float8_e4m3fn_x4
ACT = mybir.ActivationFunctionType
ALU = mybir.AluOpType

P = 128
PACK = 4
T, G, U = 1024, 2048, 1024
S = 512
FLOPS = 2 * 2 * 512 * 512 * 512


def tile_picked_pqcharmpagex_none_p_kernel(
    tc, x_words, x_scales, d_words, d_scales, gs, mem, offs, k1, n1, cand, n2, out
):
    nc = tc.nc
    with ExitStack() as ctx:
        keep = ctx.enter_context(tc.tile_pool(name="keep", bufs=1))
        psum = ctx.enter_context(tc.psum_pool(name="psum", bufs=1))

        def load_list(src, name):
            tile = keep.tile([P, S // 16], U16, name=name)
            nc.sync.dma_start(tile[:], src)
            return tile

        def dealt(ap):
            return ap.rearrange("p (t m) -> p m t", t=PACK)

        def in_order(ap):
            return ap.rearrange("p (m t) -> p m t", t=PACK)

        d_byte_table = keep.tile([P, G], U8, align_bytes=64)
        x_byte_table = keep.tile([P, T], U8, align_bytes=64)
        planes = keep.tile([P, 2 * S], U8, align_bytes=64)
        c_rows = keep.tile([P, S], U8, align_bytes=64)
        warm = keep.tile([P, 2], F32)
        nc.vector.memset(warm[:, 0:1], 1.0)
        nc.scalar.activation(warm[:, 1:2], warm[:, 0:1], ACT.Abs_reciprocal_sqrt)
        nc.vector.memset(planes[:].bitcast(I32), 0)
        nc.vector.memset(c_rows[:].bitcast(I32), 0)

        k1_list = load_list(k1, "k1_list")
        nc.sync.dma_start(d_byte_table[:].bitcast(I32), d_scales[0].bitcast(I32).unsqueeze(1).broadcast_to([16, 8, G // 4]))
        offs_list = load_list(offs, "offs_list")
        nc.sync.dma_start(x_byte_table[:].bitcast(I32), x_scales[0].bitcast(I32).unsqueeze(1).broadcast_to([16, 8, T // 4]))
        cand_list = load_list(cand, "cand_list")
        n1_list = load_list(n1, "n1_list")
        n2_list = load_list(n2, "n2_list")
        x_word_table = keep.tile([P, T], U32, align_bytes=64)
        nc.sync.dma_start(x_word_table[:].bitcast(I32), x_words[0].rearrange("p n t -> p (n t)").bitcast(I32))
        d_word_table = keep.tile([P, G], U32, align_bytes=64)
        nc.sync.dma_start(d_word_table[:].bitcast(I32), d_words[0].rearrange("p n t -> p (n t)").bitcast(I32))
        mem_rows = mem.rearrange("(p t) w -> t p w", t=PACK)
        out_rows = out.rearrange("(p t) w -> t p w", t=PACK)
        pages = []

        def load_page(slot):
            t = len(pages)
            pages.append(keep.tile([P, U], F32, name=f"page{t}", tag=slot, align_bytes=64))
            nc.sync.dma_start(pages[t][:], mem_rows[t])

        identity = keep.tile([P, P], F32)
        make_identity(nc, identity[:])

        picked_bytes = keep.tile([P, 2 * S], U8, align_bytes=64)
        nc.vector.tensor_copy(picked_bytes[:, 0:S], d_byte_table[:].indirect(k1_list[:]))
        nc.vector.tensor_copy(picked_bytes[:, S : 2 * S], x_byte_table[:].indirect(offs_list[:]))
        gain = keep.tile([P, PACK], F32, tag="d_byte_table", align_bytes=64)
        nc.sync.dma_start(gain[:], gs.rearrange("(p t) o -> p (t o)", t=PACK))
        for r in range(4):
            nc.scalar.dma_start(planes[r:P:32, :].bitcast(I32), picked_bytes[8 * r : P : 32, :].bitcast(I32))
        load_page("picked_bytes")

        xq_words = keep.tile([P, S], U32, align_bytes=64)
        nc.vector.tensor_copy(xq_words[:], x_word_table[:].indirect(offs_list[:]))
        d_picked = keep.tile([P, S], U32, align_bytes=64)
        nc.vector.tensor_copy(d_picked[:], d_word_table[:].indirect(k1_list[:]))
        d_dealt = keep.tile([P, S], U32, align_bytes=64)
        nc.vector.tensor_copy(dealt(d_dealt[:]), in_order(d_picked[:]))
        d_plane = keep.tile([P, S], U8, tag="d_word_table", align_bytes=64)
        nc.vector.tensor_copy(dealt(d_plane[:]), in_order(planes[:, 0:S]))

        h_banks = []
        for t in range(PACK):
            cols = slice(t * P, (t + 1) * P)
            bank = psum.tile([P, S], F32, name=f"h_bank{t}", tag=f"first{t}")
            nc.tensor.matmul_mx(
                out=bank[:],
                lhsT=d_dealt[:, cols].bitcast(FP8X4),
                lhsT_scale=d_plane[:, cols],
                rhs=xq_words[:].bitcast(FP8X4),
                rhs_scale=planes[:, S : 2 * S],
                start=True,
                stop=True,
            )
            h_banks.append(bank)

        c_bytes = keep.tile([P, S], U8, tag="d_picked", align_bytes=64)
        nc.vector.tensor_copy(c_bytes[:], x_byte_table[:].indirect(cand_list[:]))
        for r in range(4):
            nc.sync.dma_start(c_rows[r:P:32, :].bitcast(I32), c_bytes[8 * r : P : 32, :].bitcast(I32))
        c_picked = keep.tile([P, S], U32, tag="x_byte_table", align_bytes=64)
        nc.vector.tensor_copy(c_picked[:], x_word_table[:].indirect(cand_list[:]))
        load_page("d_dealt")
        load_page("xq_words")
        load_page("x_word_table")

        h_tiles = [keep.tile([P, 2 * S], F32, name=f"h{t}", align_bytes=64) for t in range(PACK)]
        pa = [keep.tile([P, S], F32, name=f"pa{t}", align_bytes=64) for t in range(PACK)]
        pa_sq = [keep.tile([P, S], F32, name=f"pa_sq{t}", align_bytes=64) for t in range(PACK)]
        root = [keep.tile([P, S], F32, name=f"root{t}", align_bytes=64) for t in range(PACK)]
        recip = [keep.tile([P, S], F32, name=f"recip{t}") for t in range(PACK)]
        halves = []
        sum_banks = [psum.tile([P, PACK, P], F32, name=f"sum_bank{c}", tag=f"second{c}") for c in range(PACK)]

        def evacuate(t):
            nc.scalar.activation(h_tiles[t][:, 0:S], h_banks[t][:], ACT.Copy, scale=0.0625)
            nc.scalar.activation(h_tiles[t][:, S : 2 * S], h_banks[t][:], ACT.Square, scale=0.0625)

        def look_up(t):
            nc.vector.tensor_copy(pa[t][:], h_tiles[t][:].indirect(n1_list[:]))
            nc.scalar.activation(pa_sq[t][:], pa[t][:], ACT.Square)

        def add_squares(t):
            for c in range(PACK):
                cols = slice(c * P, (c + 1) * P)
                nc.tensor.matmul(sum_banks[c][:, t, :], h_tiles[t][:, S + c * P : S + (c + 1) * P], identity[:],
                                 start=True, stop=False, is_transpose=True)
                nc.tensor.matmul(sum_banks[c][:, t, :], pa_sq[t][:, cols], identity[:],
                                 start=False, stop=True, is_transpose=True)

        def invert(t):
            nc.scalar.activation(root[t][:], sum_banks[t][:].rearrange("j t p -> j (t p)"), ACT.Abs_reciprocal_sqrt, scale=0.5, bias=0.25)
            nc.scalar.activation(recip[t][:], root[t][:], ACT.Square)

        def numerator(t):
            nc.vector.scalar_tensor_tensor(numer[:, t, :], pa[t][:], gain[:, t : t + 1], h_tiles[t][:, 0:S], ALU.mult, ALU.mult)

        def fetch_half(t, slot):
            halves.append(keep.tile([P, S], F32, name=f"half{t}", tag=slot, align_bytes=64))
            nc.vector.tensor_scalar(halves[t][:], pages[t][:].indirect(n2_list[:]), 0.5, 0.0, ALU.mult, ALU.add)

        evacuate(0)
        evacuate(1)
        for t in range(PACK):
            if t + 2 < PACK:
                evacuate(t + 2)
            look_up(t)
            add_squares(t)
        numer = keep.tile([P, PACK, S], F32, tag="pa_sq1", align_bytes=64)
        for t in range(PACK):
            numerator(t)
        fetch_half(0, "pa_sq2")
        c_dealt = keep.tile([P, S], U32, tag="pa_sq3", align_bytes=64)
        nc.vector.tensor_copy(dealt(c_dealt[:]), in_order(c_picked[:]))
        c_plane = keep.tile([P, S], U8, tag="pa0", align_bytes=64)
        nc.vector.tensor_copy(dealt(c_plane[:]), in_order(c_rows[:]))
        fetch_half(1, "pa1")

        recip_banks = [psum.tile([P, PACK, P], F32, name=f"recip_bank{c}", tag=f"first{c}") for c in range(PACK)]
        for c in range(PACK):
            invert(c)
            for t in range(PACK):
                nc.tensor.transpose(recip_banks[c][:, t, :], recip[c][:, t * P : (t + 1) * P], identity[:])

        z = [keep.tile([P, S // 2, PACK], BF16, name=f"z{i}", align_bytes=64) for i in range(2)]
        z_words = [keep.tile([P, S // 2], U32, name=f"z_words{i}", align_bytes=64) for i in range(2)]
        z_plane = [keep.tile([P, S // 2], U8, name=f"z_plane{i}", align_bytes=64) for i in range(2)]

        def finish_z(c):
            nc.vector.tensor_tensor(
                z[c // 2][:, (c % 2) * P : (c % 2 + 1) * P, :],
                numer[:, :, c * P : (c + 1) * P].rearrange("p t j -> p j t"),
                recip_banks[c][:].rearrange("p t j -> p j t"),
                ALU.mult,
            )

        def quantise(i):
            nc.vector.quantize_mx(out=z_words[i][:].bitcast(FP8X4), scales=z_plane[i][:], in_=z[i][:].rearrange("p j t -> p (j t)"))

        finish_z(0)
        finish_z(1)
        fetch_half(2, "root0")
        finish_z(2)
        quantise(0)
        finish_z(3)
        quantise(1)
        fetch_half(PACK - 1, "z1")

        s_banks = [psum.tile([P, S], F32, name=f"s_bank{t}", tag=f"second{t}") for t in range(PACK)]
        for i in range(2):
            for t in range(PACK):
                cols = slice(t * P, (t + 1) * P)
                nc.tensor.matmul_mx(
                    out=s_banks[t][:, i * (S // 2) : (i + 1) * (S // 2)],
                    lhsT=c_dealt[:, cols].bitcast(FP8X4),
                    lhsT_scale=c_plane[:, cols],
                    rhs=z_words[i][:].bitcast(FP8X4),
                    rhs_scale=z_plane[i][:],
                    start=True,
                    stop=True,
                )

        larger = [keep.tile([P, S], F32, name=f"larger{t}") for t in range(PACK)]

        def take_larger(t):
            nc.vector.scalar_tensor_tensor(larger[t][:], s_banks[t][:], 0.0625, halves[t][:], ALU.mult, ALU.max)

        take_larger(0)
        for t in range(PACK):
            if t + 1 < PACK:
                take_larger(t + 1)
            nc.vector.tensor_copy(pages[t][:].indirect(n2_list[:]), larger[t][:])
            nc.sync.dma_start(out_rows[t], pages[t][:])
